import numpy as np
import ml_dtypes


def mxq(x, axis, fmt="e4m3"):
    dtype, down = {"e4m3": (ml_dtypes.float8_e4m3fn, 7), "e5m2": (ml_dtypes.float8_e5m2, 14)}[fmt]
    v = np.moveaxis(np.asarray(x, np.float32).astype(ml_dtypes.bfloat16).astype(np.float64), axis, -1)
    blocks = v.reshape(v.shape[:-1] + (-1, 32))
    amax = np.abs(blocks).max(-1, keepdims=True)
    byte = np.maximum(np.where(amax > 0, np.frexp(amax)[1] - 1 + 127, 0) - down, 1)
    scale = np.exp2(byte - 127.0)
    codes = (blocks / scale).astype(np.float32).astype(dtype).astype(np.float64)
    return np.moveaxis((codes * scale).reshape(v.shape), -1, axis)


WIDE = False


def mx_kscale(k, group=512):
    if not WIDE:
        return np.ones(k)
    levels = np.array([18, -18])
    if group != 512:
        return np.exp2(np.random.permutation(np.resize(levels, k // group))).repeat(group)
    if k % 512:
        return np.exp2(np.random.permutation(np.resize(levels, k // 32))).repeat(32)
    a = np.empty((k // 512, 16))
    for p in range(k // 512):
        a[p, :8] = np.random.permutation(np.resize(levels, 8))
        for g in range(8):
            far = levels[np.abs(levels - a[p, g]) >= 10]
            a[p, g + 8] = far[np.random.randint(len(far))]
    return np.exp2(a.ravel()).repeat(32)


def f64(x):
    return np.asarray(x).astype(np.float64)


G, D, M, O, N = 4, 128, 128, 128, 512


def sgn(shape):
    return np.random.uniform(0.5, 2.0, shape) * np.where(np.random.standard_normal(shape) < 0, -1.0, 1.0)


def setup_inputs():
    n = np.random.standard_normal
    s_d = mx_kscale(D, 0)
    s_m = mx_kscale(M, 0)
    return {
        "x": (n((G, D, N)) * s_d[:, None]).astype(np.float32),
        "w1": (n((G, D, M)) / np.sqrt(D) / s_d[:, None]).astype(np.float32),
        "w2": (n((G, D, M)) / np.sqrt(D) / s_d[:, None]).astype(np.float32),
        "tp": (np.random.uniform(0.6, 2.0, (G, M, 1))).astype(np.float32),
        "hs": (sgn((G, M, 1)) * s_m[:, None]).astype(np.float32),
        "wo2": (n((G, M, O)) / np.sqrt(M) / s_m[:, None]).astype(np.float32),
        "res": (0.5 * n((G, O, N))).astype(np.float32),
    }


def reference(x, w1, w2, tp, hs, wo2, res):
    w1q = mxq(f64(w1), 1, "e4m3")
    xq = mxq(f64(x), 1, "e4m3")
    z1 = w1q.transpose(0, 2, 1) @ xq
    w2q = mxq(f64(w2), 1, "e4m3")
    z2 = w2q.transpose(0, 2, 1) @ xq
    se = np.exp(z1 * f64(tp)) + np.exp(z2 * f64(tp))
    h = np.log(se) / f64(tp)
    hh = h * f64(hs)
    wo2q = mxq(f64(wo2), 1, "e4m3")
    hhq = mxq(hh, 1, "e4m3")
    y0 = wo2q.transpose(0, 2, 1) @ hhq
    y = y0 + f64(res)
    return y

@@ -1,0 +1,192 @@
+from contextlib import ExitStack
+
+import concourse.mybir as mybir
+
+G, D, M, O, N = 4, 128, 128, 128, 512
+FLOPS = 2 * G * N * (2 * D * M + M * O)
+
+F32 = mybir.dt.float32
+BF16 = mybir.dt.bfloat16
+U32 = mybir.dt.uint32
+U8 = mybir.dt.uint8
+FP8X4 = mybir.dt.float8_e4m3fn_x4
+ALU = mybir.AluOpType
+ACT = mybir.ActivationFunctionType
+
+P = 128
+PACK = 4
+ROWS = 32
+NC = 128
+HALF = 256
+CLAMP = 32.0
+
+
+def side_by_side(words, rows):
+    return (
+        words.rearrange("p (c i) j -> p c j i", i=4),
+        rows.rearrange("p j (c i) -> p c j i", i=4),
+    )
+
+
+def quantize(nc, codes, scales, words):
+    nc.vector.quantize_mx(
+        out=codes.bitcast(FP8X4), scales=scales, in_=words.rearrange("p n j -> p (n j)")
+    )
+
+
+def row_tile_matmul(nc, out, g, w, w_col, a, a_col, start, stop):
+    rows = slice(ROWS * g, ROWS * (g + 1))
+    wc = slice(w_col, w_col + NC)
+    ac = slice(a_col, a_col + NC)
+    nc.tensor.matmul_mx(
+        out=out,
+        lhsT=w[0][rows, wc].bitcast(FP8X4),
+        lhsT_scale=w[1][rows, wc],
+        rhs=a[0][rows, ac].bitcast(FP8X4),
+        rhs_scale=a[1][rows, ac],
+        start=start,
+        stop=stop,
+    )
+
+
+def tile_rows_fsoftmaxoftwo_kernel(tc, x, w1, w2, tp, hs, wo2, res, out):
+    nc = tc.nc
+    halves = range(N // HALF)
+    groups = range(G)
+
+    with ExitStack() as ctx:
+        sb = ctx.enter_context(tc.tile_pool(name="sb", bufs=1))
+        ps = ctx.enter_context(tc.psum_pool(name="ps", bufs=1))
+        ctx.enter_context(tc.manual_schedule())
+
+        def tile(name, shape, dtype):
+            return sb.tile(shape, dtype, name=name, align_bytes=64)
+
+        def planes(name, width):
+            return (tile(name + "_codes", [P, width], U32), tile(name + "_scales", [P, width], U8))
+
+        def k_rows(t):
+            return t.rearrange("g (p j) n -> (g p) j n", j=PACK)
+
+        vec_rows = tile("vec_rows", [P, P], F32)
+        nc.gpsimd.memset(vec_rows[:], 1.0)
+        w2_raw = tile("w2_raw", [P, PACK, M], F32)
+        w1_raw = tile("w1_raw", [P, PACK, M], F32)
+        x_raw = [tile("x_raw%d" % h, [P, PACK, HALF], F32) for h in halves]
+        wo_raw = tile("wo_raw", [P, PACK, O], F32)
+        res_sb = tile("res_sb", [P, G, N], F32)
+        nc.sync.dma_start(out=w2_raw[:], in_=k_rows(w2))
+        nc.sync.dma_start(out=w1_raw[:], in_=k_rows(w1))
+        for row, vec in enumerate((tp, hs)):
+            nc.scalar.dma_start(
+                out=vec_rows[row:P:ROWS, :].rearrange("a (g k) -> a g k", g=G),
+                in_=vec.rearrange("g (a k) o -> a g (k o)", k=ROWS),
+            )
+        for h in halves:
+            nc.sync.dma_start(out=x_raw[h][:], in_=k_rows(x)[:, :, h * HALF : (h + 1) * HALF])
+        nc.sync.dma_start(out=wo_raw[:], in_=k_rows(wo2))
+        nc.sync.dma_start(out=res_sb[:], in_=res.rearrange("g o n -> o g n"))
+
+        w_words = tile("w_words", [P, 2 * M, PACK], BF16)
+        dst, src = side_by_side(w_words[:, 0:M, :], w2_raw[:])
+        nc.vector.tensor_copy(out=dst, in_=src)
+        dst, src = side_by_side(w_words[:, M : 2 * M, :], w1_raw[:])
+        nc.vector.tensor_scalar(out=dst, in0=src, scalar1=-1.0, scalar2=None, op0=ALU.mult)
+        vec_cols = tile("vec_cols", [P, P], F32)
+        nc.vector.transpose(vec_cols[:], vec_rows[:])
+        w_mx = planes("w", 2 * M)
+        quantize(nc, w_mx[0][:], w_mx[1][:], w_words[:])
+        inv_tp = tile("inv_tp", [P, G], F32)
+        ratio = tile("ratio", [P, G], F32)
+        nc.vector.reciprocal(out=inv_tp[:], in_=vec_cols[:, 0:P:ROWS])
+        tp_col = [vec_cols[:, ROWS * g : ROWS * g + 1] for g in groups]
+        hs_col = [vec_cols[:, ROWS * g + 1 : ROWS * g + 2] for g in groups]
+        ratio_col = [ratio[:, g : g + 1] for g in groups]
+
+        x_mx = [planes("x%d" % h, HALF) for h in halves]
+        banks = [[ps.tile([P, 2, HALF], F32, name="bank%d_%d" % (g, h)) for h in halves] for g in groups]
+
+        def prepare(words, raw):
+            dst, src = side_by_side(words[:, NC:HALF, :], raw[:, :, NC:HALF])
+            nc.scalar.copy(out=dst, in_=src)
+            dst, src = side_by_side(words[:, 0:NC, :], raw[:, :, 0:NC])
+            nc.vector.tensor_copy(out=dst, in_=src)
+
+        def diff_matmuls(h):
+            for c in range(0, HALF, NC):
+                for w_col in (0, M):
+                    for g in groups:
+                        row_tile_matmul(nc, banks[g][h][:, 0, c : c + NC], g, w_mx, w_col, x_mx[h], c, w_col == 0, w_col == M)
+
+        def z2_matmuls(h):
+            for c in range(0, HALF, NC):
+                for g in groups:
+                    row_tile_matmul(nc, banks[g][h][:, 1, c : c + NC], g, w_mx, 0, x_mx[h], c, True, True)
+
+        for h in halves:
+            x_words = tile("x_words%d" % h, [P, HALF, PACK], BF16)
+            prepare(x_words, x_raw[h])
+            if h == 0:
+                nc.vector.tensor_tensor(out=ratio[:], in0=inv_tp[:], in1=vec_cols[:, 1:P:ROWS], op=ALU.mult)
+            quantize(nc, x_mx[h][0][:], x_mx[h][1][:], x_words[:])
+            diff_matmuls(h)
+
+        q = [tile("q%d" % h, [P, G, HALF], F32) for h in halves]
+        cq = [tile("cq%d" % h, [P, G, HALF], F32) for h in halves]
+        e = [tile("e%d" % h, [P, G, HALF], F32) for h in halves]
+        for h in halves:
+            for g in groups:
+                nc.vector.tensor_scalar(
+                    out=q[h][:, g, :], in0=banks[g][h][:, 0, :], scalar1=tp_col[g], scalar2=CLAMP, op0=ALU.mult, op1=ALU.min
+                )
+                nc.gpsimd.tensor_scalar(
+                    out=cq[h][:, g, :], in0=q[h][:, g, :], scalar1=ratio_col[g], scalar2=0.0, op0=ALU.mult, op1=ALU.add
+                )
+                if g % 2 == 1:
+                    nc.scalar.activation(out=e[h][:, g - 1 : g + 1, :], in_=q[h][:, g - 1 : g + 1, :], func=ACT.Exp)
+            z2_matmuls(h)
+
+        base = [tile("base%d" % h, [P, G, HALF], F32) for h in halves]
+        for h in halves:
+            for g in groups:
+                nc.vector.scalar_tensor_tensor(
+                    out=base[h][:, g, :], in0=banks[g][h][:, 1, :], scalar=hs_col[g], in1=cq[h][:, g, :], op0=ALU.mult, op1=ALU.subtract
+                )
+
+        lg = [tile("lg%d" % h, [P, G, HALF], F32) for h in halves]
+        hh_rows = [tile("hh_rows%d" % h, [P, PACK, HALF], BF16) for h in halves]
+        for h in halves:
+            for g in groups:
+                if g % 2 == 0:
+                    nc.scalar.activation(out=lg[h][:, g : g + 2, :], in_=e[h][:, g : g + 2, :], func=ACT.Ln, bias=1.0)
+                hh = tile("hh%d_%d" % (h, g), [P, HALF], BF16)
+                nc.vector.scalar_tensor_tensor(
+                    out=hh[:], in0=lg[h][:, g, :], scalar=ratio_col[g], in1=base[h][:, g, :], op0=ALU.mult, op1=ALU.add
+                )
+                nc.sync.dma_start(out=hh_rows[h][ROWS * g : ROWS * (g + 1), :, :], in_=hh[:])
+
+        wo_words = tile("wo_words", [P, O, PACK], BF16)
+        dst, src = side_by_side(wo_words[:], wo_raw[:])
+        nc.scalar.copy(out=dst, in_=src)
+        wo_mx = planes("wo", O)
+        quantize(nc, wo_mx[0][:], wo_mx[1][:], wo_words[:])
+
+        out_view = out.rearrange("g o n -> o g n")
+        for h in halves:
+            hh_words = tile("hh_words%d" % h, [P, HALF, PACK], BF16)
+            if h == 0:
+                prepare(hh_words, hh_rows[h])
+            else:
+                dst, src = side_by_side(hh_words[:], hh_rows[h][:])
+                nc.scalar.copy(out=dst, in_=src)
+            hh_mx = planes("hh%d" % h, HALF)
+            quantize(nc, hh_mx[0][:], hh_mx[1][:], hh_words[:])
+            for c in range(0, HALF, NC):
+                for g in groups:
+                    row_tile_matmul(nc, banks[g][h][:, 0, c : c + NC], g, wo_mx, 0, hh_mx, c, True, True)
+            cols = slice(h * HALF, (h + 1) * HALF)
+            for g0 in range(0, G, 2):
+                y = tile("y%d_%d" % (h, g0), [P, 2, HALF], F32)
+                for g in (g0, g0 + 1):
+                    nc.vector.tensor_tensor(out=y[:, g - g0, :], in0=banks[g][h][:, 0, :], in1=res_sb[:, g, cols], op=ALU.add)
+                nc.sync.dma_start(out=out_view[:, g0 : g0 + 2, cols], in_=y[:])

@@ -75,61 +75,71 @@ def tile_rows_fsoftmaxoftwo_kernel(tc, x, w1, w2, tp, hs, wo2, res, out):
         x_raw = [tile("x_raw%d" % h, [P, PACK, HALF], F32) for h in halves]
         wo_raw = tile("wo_raw", [P, PACK, O], F32)
         res_sb = tile("res_sb", [P, G, N], F32)
-        nc.sync.dma_start(out=w2_raw[:], in_=k_rows(w2))
-        nc.sync.dma_start(out=w1_raw[:], in_=k_rows(w1))
         for row, vec in enumerate((tp, hs)):
-            nc.scalar.dma_start(
+            nc.sync.dma_start(
                 out=vec_rows[row:P:ROWS, :].rearrange("a (g k) -> a g k", g=G),
                 in_=vec.rearrange("g (a k) o -> a g (k o)", k=ROWS),
             )
-        for h in halves:
-            nc.sync.dma_start(out=x_raw[h][:], in_=k_rows(x)[:, :, h * HALF : (h + 1) * HALF])
+        nc.sync.dma_start(out=x_raw[0][:], in_=k_rows(x)[:, :, 0:HALF])
+        nc.sync.dma_start(out=w2_raw[:], in_=k_rows(w2))
+        nc.sync.dma_start(out=w1_raw[:], in_=k_rows(w1))
+        nc.sync.dma_start(out=x_raw[1][:], in_=k_rows(x)[:, :, HALF:N])
         nc.sync.dma_start(out=wo_raw[:], in_=k_rows(wo2))
         nc.sync.dma_start(out=res_sb[:], in_=res.rearrange("g o n -> o g n"))
 
-        w_words = tile("w_words", [P, 2 * M, PACK], BF16)
-        dst, src = side_by_side(w_words[:, 0:M, :], w2_raw[:])
-        nc.vector.tensor_copy(out=dst, in_=src)
-        dst, src = side_by_side(w_words[:, M : 2 * M, :], w1_raw[:])
-        nc.vector.tensor_scalar(out=dst, in0=src, scalar1=-1.0, scalar2=None, op0=ALU.mult)
         vec_cols = tile("vec_cols", [P, P], F32)
-        nc.vector.transpose(vec_cols[:], vec_rows[:])
-        w_mx = planes("w", 2 * M)
-        quantize(nc, w_mx[0][:], w_mx[1][:], w_words[:])
         inv_tp = tile("inv_tp", [P, G], F32)
         ratio = tile("ratio", [P, G], F32)
+        nc.vector.transpose(vec_cols[:], vec_rows[:])
         nc.vector.reciprocal(out=inv_tp[:], in_=vec_cols[:, 0:P:ROWS])
+        nc.vector.tensor_tensor(out=ratio[:], in0=inv_tp[:], in1=vec_cols[:, 1:P:ROWS], op=ALU.mult)
         tp_col = [vec_cols[:, ROWS * g : ROWS * g + 1] for g in groups]
         hs_col = [vec_cols[:, ROWS * g + 1 : ROWS * g + 2] for g in groups]
         ratio_col = [ratio[:, g : g + 1] for g in groups]
 
         x_mx = [planes("x%d" % h, HALF) for h in halves]
+        w_mx = [planes("w2", M), planes("w1", M)]
         banks = [[ps.tile([P, 2, HALF], F32, name="bank%d_%d" % (g, h)) for h in halves] for g in groups]
 
-        def prepare(words, raw):
-            dst, src = side_by_side(words[:, NC:HALF, :], raw[:, :, NC:HALF])
-            nc.scalar.copy(out=dst, in_=src)
-            dst, src = side_by_side(words[:, 0:NC, :], raw[:, :, 0:NC])
+        def vector_words(words, raw):
+            dst, src = side_by_side(words, raw)
             nc.vector.tensor_copy(out=dst, in_=src)
+
+        def scalar_words(words, raw):
+            dst, src = side_by_side(words, raw)
+            nc.scalar.copy(out=dst, in_=src)
+
+        def prepare(words, raw):
+            scalar_words(words[:, NC:HALF, :], raw[:, :, NC:HALF])
+            vector_words(words[:, 0:NC, :], raw[:, :, 0:NC])
 
         def diff_matmuls(h):
             for c in range(0, HALF, NC):
-                for w_col in (0, M):
+                for i in range(2):
                     for g in groups:
-                        row_tile_matmul(nc, banks[g][h][:, 0, c : c + NC], g, w_mx, w_col, x_mx[h], c, w_col == 0, w_col == M)
+                        row_tile_matmul(nc, banks[g][h][:, 0, c : c + NC], g, w_mx[i], 0, x_mx[h], c, i == 0, i == 1)
 
         def z2_matmuls(h):
             for c in range(0, HALF, NC):
                 for g in groups:
-                    row_tile_matmul(nc, banks[g][h][:, 1, c : c + NC], g, w_mx, 0, x_mx[h], c, True, True)
+                    row_tile_matmul(nc, banks[g][h][:, 1, c : c + NC], g, w_mx[0], 0, x_mx[h], c, True, True)
 
-        for h in halves:
-            x_words = tile("x_words%d" % h, [P, HALF, PACK], BF16)
-            prepare(x_words, x_raw[h])
-            if h == 0:
-                nc.vector.tensor_tensor(out=ratio[:], in0=inv_tp[:], in1=vec_cols[:, 1:P:ROWS], op=ALU.mult)
-            quantize(nc, x_mx[h][0][:], x_mx[h][1][:], x_words[:])
-            diff_matmuls(h)
+        x_words = [tile("x_words%d" % h, [P, HALF, PACK], BF16) for h in halves]
+        w2_words = tile("w2_words", [P, M, PACK], BF16)
+        w1_words = tile("w1_words", [P, M, PACK], BF16)
+        prepare(x_words[0], x_raw[0])
+        vector_words(w2_words[:], w2_raw[:])
+        quantize(nc, x_mx[0][0][:], x_mx[0][1][:], x_words[0][:])
+        quantize(nc, w_mx[0][0][:], w_mx[0][1][:], w2_words[:])
+        dst, src = side_by_side(w1_words[:, 0:64, :], w1_raw[:, :, 0:64])
+        nc.vector.tensor_scalar(out=dst, in0=src, scalar1=-1.0, scalar2=None, op0=ALU.mult)
+        dst, src = side_by_side(w1_words[:, 64:M, :], w1_raw[:, :, 64:M])
+        nc.scalar.activation(out=dst, in_=src, func=ACT.Copy, scale=-1.0)
+        quantize(nc, w_mx[1][0][:], w_mx[1][1][:], w1_words[:])
+        diff_matmuls(0)
+        prepare(x_words[1], x_raw[1])
+        quantize(nc, x_mx[1][0][:], x_mx[1][1][:], x_words[1][:])
+        diff_matmuls(1)
 
         q = [tile("q%d" % h, [P, G, HALF], F32) for h in halves]
         cq = [tile("cq%d" % h, [P, G, HALF], F32) for h in halves]
@@ -142,8 +152,7 @@ def tile_rows_fsoftmaxoftwo_kernel(tc, x, w1, w2, tp, hs, wo2, res, out):
                 nc.gpsimd.tensor_scalar(
                     out=cq[h][:, g, :], in0=q[h][:, g, :], scalar1=ratio_col[g], scalar2=0.0, op0=ALU.mult, op1=ALU.add
                 )
-                if g % 2 == 1:
-                    nc.scalar.activation(out=e[h][:, g - 1 : g + 1, :], in_=q[h][:, g - 1 : g + 1, :], func=ACT.Exp)
+                nc.scalar.activation(out=e[h][:, g, :], in_=q[h][:, g, :], func=ACT.Exp)
             z2_matmuls(h)
 
         base = [tile("base%d" % h, [P, G, HALF], F32) for h in halves]
@@ -157,8 +166,7 @@ def tile_rows_fsoftmaxoftwo_kernel(tc, x, w1, w2, tp, hs, wo2, res, out):
         hh_rows = [tile("hh_rows%d" % h, [P, PACK, HALF], BF16) for h in halves]
         for h in halves:
             for g in groups:
-                if g % 2 == 0:
-                    nc.scalar.activation(out=lg[h][:, g : g + 2, :], in_=e[h][:, g : g + 2, :], func=ACT.Ln, bias=1.0)
+                nc.scalar.activation(out=lg[h][:, g, :], in_=e[h][:, g, :], func=ACT.Ln, bias=1.0)
                 hh = tile("hh%d_%d" % (h, g), [P, HALF], BF16)
                 nc.vector.scalar_tensor_tensor(
                     out=hh[:], in0=lg[h][:, g, :], scalar=ratio_col[g], in1=base[h][:, g, :], op0=ALU.mult, op1=ALU.add
@@ -172,21 +180,27 @@ def tile_rows_fsoftmaxoftwo_kernel(tc, x, w1, w2, tp, hs, wo2, res, out):
         quantize(nc, wo_mx[0][:], wo_mx[1][:], wo_words[:])
 
         out_view = out.rearrange("g o n -> o g n")
-        for h in halves:
-            hh_words = tile("hh_words%d" % h, [P, HALF, PACK], BF16)
-            if h == 0:
-                prepare(hh_words, hh_rows[h])
-            else:
-                dst, src = side_by_side(hh_words[:], hh_rows[h][:])
-                nc.scalar.copy(out=dst, in_=src)
-            hh_mx = planes("hh%d" % h, HALF)
-            quantize(nc, hh_mx[0][:], hh_mx[1][:], hh_words[:])
+        hh_words = [tile("hh_words%d" % h, [P, HALF, PACK], BF16) for h in halves]
+        hh_mx = [planes("hh%d" % h, HALF) for h in halves]
+
+        def second_layer(h):
+            quantize(nc, hh_mx[h][0][:], hh_mx[h][1][:], hh_words[h][:])
             for c in range(0, HALF, NC):
                 for g in groups:
-                    row_tile_matmul(nc, banks[g][h][:, 0, c : c + NC], g, wo_mx, 0, hh_mx, c, True, True)
+                    row_tile_matmul(nc, banks[g][h][:, 0, c : c + NC], g, wo_mx, 0, hh_mx[h], c, True, True)
+
+        def finish(h, g):
             cols = slice(h * HALF, (h + 1) * HALF)
-            for g0 in range(0, G, 2):
-                y = tile("y%d_%d" % (h, g0), [P, 2, HALF], F32)
-                for g in (g0, g0 + 1):
-                    nc.vector.tensor_tensor(out=y[:, g - g0, :], in0=banks[g][h][:, 0, :], in1=res_sb[:, g, cols], op=ALU.add)
-                nc.sync.dma_start(out=out_view[:, g0 : g0 + 2, cols], in_=y[:])
+            y = tile("y%d_%d" % (h, g), [P, HALF], F32)
+            nc.vector.tensor_tensor(out=y[:], in0=banks[g][h][:, 0, :], in1=res_sb[:, g, cols], op=ALU.add)
+            nc.sync.dma_start(out=out_view[:, g, cols], in_=y[:])
+
+        prepare(hh_words[0], hh_rows[0])
+        second_layer(0)
+        prepare(hh_words[1], hh_rows[1])
+        finish(0, 0)
+        second_layer(1)
+        for g in range(1, G):
+            finish(0, g)
+        for g in groups:
+            finish(1, g)

@@ -75,12 +75,12 @@ def tile_rows_fsoftmaxoftwo_kernel(tc, x, w1, w2, tp, hs, wo2, res, out):
         x_raw = [tile("x_raw%d" % h, [P, PACK, HALF], F32) for h in halves]
         wo_raw = tile("wo_raw", [P, PACK, O], F32)
         res_sb = tile("res_sb", [P, G, N], F32)
+        nc.sync.dma_start(out=x_raw[0][:], in_=k_rows(x)[:, :, 0:HALF])
         for row, vec in enumerate((tp, hs)):
             nc.sync.dma_start(
                 out=vec_rows[row:P:ROWS, :].rearrange("a (g k) -> a g k", g=G),
                 in_=vec.rearrange("g (a k) o -> a g (k o)", k=ROWS),
             )
-        nc.sync.dma_start(out=x_raw[0][:], in_=k_rows(x)[:, :, 0:HALF])
         nc.sync.dma_start(out=w2_raw[:], in_=k_rows(w2))
         nc.sync.dma_start(out=w1_raw[:], in_=k_rows(w1))
         nc.sync.dma_start(out=x_raw[1][:], in_=k_rows(x)[:, :, HALF:N])
@@ -90,9 +90,6 @@ def tile_rows_fsoftmaxoftwo_kernel(tc, x, w1, w2, tp, hs, wo2, res, out):
         vec_cols = tile("vec_cols", [P, P], F32)
         inv_tp = tile("inv_tp", [P, G], F32)
         ratio = tile("ratio", [P, G], F32)
-        nc.vector.transpose(vec_cols[:], vec_rows[:])
-        nc.vector.reciprocal(out=inv_tp[:], in_=vec_cols[:, 0:P:ROWS])
-        nc.vector.tensor_tensor(out=ratio[:], in0=inv_tp[:], in1=vec_cols[:, 1:P:ROWS], op=ALU.mult)
         tp_col = [vec_cols[:, ROWS * g : ROWS * g + 1] for g in groups]
         hs_col = [vec_cols[:, ROWS * g + 1 : ROWS * g + 2] for g in groups]
         ratio_col = [ratio[:, g : g + 1] for g in groups]
@@ -127,33 +124,42 @@ def tile_rows_fsoftmaxoftwo_kernel(tc, x, w1, w2, tp, hs, wo2, res, out):
         x_words = [tile("x_words%d" % h, [P, HALF, PACK], BF16) for h in halves]
         w2_words = tile("w2_words", [P, M, PACK], BF16)
         w1_words = tile("w1_words", [P, M, PACK], BF16)
+        q = [tile("q%d" % h, [P, G, HALF], F32) for h in halves]
+        cq = [tile("cq%d" % h, [P, G, HALF], F32) for h in halves]
+        e = [tile("e%d" % h, [P, G, HALF], F32) for h in halves]
+
+        def clamp_and_exp(h, g):
+            nc.vector.tensor_scalar(
+                out=q[h][:, g, :], in0=banks[g][h][:, 0, :], scalar1=tp_col[g], scalar2=CLAMP, op0=ALU.mult, op1=ALU.min
+            )
+            nc.gpsimd.tensor_scalar(
+                out=cq[h][:, g, :], in0=q[h][:, g, :], scalar1=ratio_col[g], scalar2=0.0, op0=ALU.mult, op1=ALU.add
+            )
+            nc.scalar.activation(out=e[h][:, g, :], in_=q[h][:, g, :], func=ACT.Exp)
+
         prepare(x_words[0], x_raw[0])
-        vector_words(w2_words[:], w2_raw[:])
+        scalar_words(w2_words[:], w2_raw[:])
+        nc.vector.transpose(vec_cols[:], vec_rows[:])
         quantize(nc, x_mx[0][0][:], x_mx[0][1][:], x_words[0][:])
-        quantize(nc, w_mx[0][0][:], w_mx[0][1][:], w2_words[:])
+        nc.vector.reciprocal(out=inv_tp[:], in_=vec_cols[:, 0:P:ROWS])
         dst, src = side_by_side(w1_words[:, 0:64, :], w1_raw[:, :, 0:64])
         nc.vector.tensor_scalar(out=dst, in0=src, scalar1=-1.0, scalar2=None, op0=ALU.mult)
         dst, src = side_by_side(w1_words[:, 64:M, :], w1_raw[:, :, 64:M])
         nc.scalar.activation(out=dst, in_=src, func=ACT.Copy, scale=-1.0)
+        quantize(nc, w_mx[0][0][:], w_mx[0][1][:], w2_words[:])
         quantize(nc, w_mx[1][0][:], w_mx[1][1][:], w1_words[:])
+        nc.vector.tensor_tensor(out=ratio[:], in0=inv_tp[:], in1=vec_cols[:, 1:P:ROWS], op=ALU.mult)
         diff_matmuls(0)
         prepare(x_words[1], x_raw[1])
+        clamp_and_exp(0, 0)
         quantize(nc, x_mx[1][0][:], x_mx[1][1][:], x_words[1][:])
         diff_matmuls(1)
-
-        q = [tile("q%d" % h, [P, G, HALF], F32) for h in halves]
-        cq = [tile("cq%d" % h, [P, G, HALF], F32) for h in halves]
-        e = [tile("e%d" % h, [P, G, HALF], F32) for h in halves]
-        for h in halves:
-            for g in groups:
-                nc.vector.tensor_scalar(
-                    out=q[h][:, g, :], in0=banks[g][h][:, 0, :], scalar1=tp_col[g], scalar2=CLAMP, op0=ALU.mult, op1=ALU.min
-                )
-                nc.gpsimd.tensor_scalar(
-                    out=cq[h][:, g, :], in0=q[h][:, g, :], scalar1=ratio_col[g], scalar2=0.0, op0=ALU.mult, op1=ALU.add
-                )
-                nc.scalar.activation(out=e[h][:, g, :], in_=q[h][:, g, :], func=ACT.Exp)
-            z2_matmuls(h)
+        for g in range(1, G):
+            clamp_and_exp(0, g)
+        z2_matmuls(0)
+        for g in groups:
+            clamp_and_exp(1, g)
+        z2_matmuls(1)
 
         base = [tile("base%d" % h, [P, G, HALF], F32) for h in halves]
         for h in halves:
@@ -195,12 +201,22 @@ def tile_rows_fsoftmaxoftwo_kernel(tc, x, w1, w2, tp, hs, wo2, res, out):
             nc.vector.tensor_tensor(out=y[:], in0=banks[g][h][:, 0, :], in1=res_sb[:, g, cols], op=ALU.add)
             nc.sync.dma_start(out=out_view[:, g, cols], in_=y[:])
 
+        def finish_off_vector(h, g):
+            cols = slice(h * HALF, (h + 1) * HALF)
+            y0 = tile("y0_%d_%d" % (h, g), [P, HALF], F32)
+            y = tile("y%d_%d" % (h, g), [P, HALF], F32)
+            nc.scalar.copy(out=y0[:], in_=banks[g][h][:, 0, :])
+            nc.gpsimd.tensor_tensor(out=y[:], in0=y0[:], in1=res_sb[:, g, cols], op=ALU.add)
+            return lambda: nc.scalar.dma_start(out=out_view[:, g, cols], in_=y[:])
+
         prepare(hh_words[0], hh_rows[0])
         second_layer(0)
         prepare(hh_words[1], hh_rows[1])
-        finish(0, 0)
         second_layer(1)
-        for g in range(1, G):
+        stores = [finish_off_vector(0, g) for g in (2, 3)]
+        for store in stores:
+            store()
+        for g in (0, 1):
             finish(0, g)
         for g in groups:
             finish(1, g)

from contextlib import ExitStack

import concourse.mybir as mybir

G, D, M, O, N = 4, 128, 128, 128, 512
FLOPS = 2 * G * N * (2 * D * M + M * O)

F32 = mybir.dt.float32
BF16 = mybir.dt.bfloat16
U32 = mybir.dt.uint32
U8 = mybir.dt.uint8
FP8X4 = mybir.dt.float8_e4m3fn_x4
ALU = mybir.AluOpType
ACT = mybir.ActivationFunctionType

P = 128
PACK = 4
ROWS = 32
NC = 128
HALF = 256
CLAMP = 32.0


def side_by_side(words, rows):
    return (
        words.rearrange("p (c i) j -> p c j i", i=4),
        rows.rearrange("p j (c i) -> p c j i", i=4),
    )


def quantize(nc, codes, scales, words):
    nc.vector.quantize_mx(
        out=codes.bitcast(FP8X4), scales=scales, in_=words.rearrange("p n j -> p (n j)")
    )


def row_tile_matmul(nc, out, g, w, w_col, a, a_col, start, stop):
    rows = slice(ROWS * g, ROWS * (g + 1))
    wc = slice(w_col, w_col + NC)
    ac = slice(a_col, a_col + NC)
    nc.tensor.matmul_mx(
        out=out,
        lhsT=w[0][rows, wc].bitcast(FP8X4),
        lhsT_scale=w[1][rows, wc],
        rhs=a[0][rows, ac].bitcast(FP8X4),
        rhs_scale=a[1][rows, ac],
        start=start,
        stop=stop,
    )


def tile_rows_fsoftmaxoftwo_kernel(tc, x, w1, w2, tp, hs, wo2, res, out):
    nc = tc.nc
    halves = range(N // HALF)
    groups = range(G)

    with ExitStack() as ctx:
        sb = ctx.enter_context(tc.tile_pool(name="sb", bufs=1))
        ps = ctx.enter_context(tc.psum_pool(name="ps", bufs=1))
        ctx.enter_context(tc.manual_schedule())

        def tile(name, shape, dtype):
            return sb.tile(shape, dtype, name=name, align_bytes=64)

        def planes(name, width):
            return (tile(name + "_codes", [P, width], U32), tile(name + "_scales", [P, width], U8))

        def k_rows(t):
            return t.rearrange("g (p j) n -> (g p) j n", j=PACK)

        vec_rows = tile("vec_rows", [P, P], F32)
        nc.gpsimd.memset(vec_rows[:], 1.0)
        w2_raw = tile("w2_raw", [P, PACK, M], F32)
        w1_raw = tile("w1_raw", [P, PACK, M], F32)
        x_raw = [tile("x_raw%d" % h, [P, PACK, HALF], F32) for h in halves]
        wo_raw = tile("wo_raw", [P, PACK, O], F32)
        res_sb = tile("res_sb", [P, G, N], F32)
        nc.sync.dma_start(out=x_raw[0][:], in_=k_rows(x)[:, :, 0:HALF])
        for row, vec in enumerate((tp, hs)):
            nc.sync.dma_start(
                out=vec_rows[row:P:ROWS, :].rearrange("a (g k) -> a g k", g=G),
                in_=vec.rearrange("g (a k) o -> a g (k o)", k=ROWS),
            )
        nc.sync.dma_start(out=w2_raw[:], in_=k_rows(w2))
        nc.sync.dma_start(out=w1_raw[:], in_=k_rows(w1))
        nc.sync.dma_start(out=x_raw[1][:], in_=k_rows(x)[:, :, HALF:N])
        nc.sync.dma_start(out=wo_raw[:], in_=k_rows(wo2))
        nc.sync.dma_start(out=res_sb[:], in_=res.rearrange("g o n -> o g n"))

        vec_cols = tile("vec_cols", [P, P], F32)
        inv_tp = tile("inv_tp", [P, G], F32)
        ratio = tile("ratio", [P, G], F32)
        tp_col = [vec_cols[:, ROWS * g : ROWS * g + 1] for g in groups]
        hs_col = [vec_cols[:, ROWS * g + 1 : ROWS * g + 2] for g in groups]
        ratio_col = [ratio[:, g : g + 1] for g in groups]

        x_mx = [planes("x%d" % h, HALF) for h in halves]
        w_mx = [planes("w2", M), planes("w1", M)]
        banks = [[ps.tile([P, 2, HALF], F32, name="bank%d_%d" % (g, h)) for h in halves] for g in groups]

        def vector_words(words, raw):
            dst, src = side_by_side(words, raw)
            nc.vector.tensor_copy(out=dst, in_=src)

        def scalar_words(words, raw):
            dst, src = side_by_side(words, raw)
            nc.scalar.copy(out=dst, in_=src)

        def prepare(words, raw):
            scalar_words(words[:, NC:HALF, :], raw[:, :, NC:HALF])
            vector_words(words[:, 0:NC, :], raw[:, :, 0:NC])

        def diff_matmuls(h):
            for c in range(0, HALF, NC):
                for i in range(2):
                    for g in groups:
                        row_tile_matmul(nc, banks[g][h][:, 0, c : c + NC], g, w_mx[i], 0, x_mx[h], c, i == 0, i == 1)

        def z2_matmuls(h):
            for c in range(0, HALF, NC):
                for g in groups:
                    row_tile_matmul(nc, banks[g][h][:, 1, c : c + NC], g, w_mx[0], 0, x_mx[h], c, True, True)

        x_words = [tile("x_words%d" % h, [P, HALF, PACK], BF16) for h in halves]
        w2_words = tile("w2_words", [P, M, PACK], BF16)
        w1_words = tile("w1_words", [P, M, PACK], BF16)
        q = [tile("q%d" % h, [P, G, HALF], F32) for h in halves]
        cq = [tile("cq%d" % h, [P, G, HALF], F32) for h in halves]
        e = [tile("e%d" % h, [P, G, HALF], F32) for h in halves]

        def clamp_and_exp(h, g):
            nc.vector.tensor_scalar(
                out=q[h][:, g, :], in0=banks[g][h][:, 0, :], scalar1=tp_col[g], scalar2=CLAMP, op0=ALU.mult, op1=ALU.min
            )
            nc.gpsimd.tensor_scalar(
                out=cq[h][:, g, :], in0=q[h][:, g, :], scalar1=ratio_col[g], scalar2=0.0, op0=ALU.mult, op1=ALU.add
            )
            nc.scalar.activation(out=e[h][:, g, :], in_=q[h][:, g, :], func=ACT.Exp)

        prepare(x_words[0], x_raw[0])
        scalar_words(w2_words[:], w2_raw[:])
        nc.vector.transpose(vec_cols[:], vec_rows[:])
        quantize(nc, x_mx[0][0][:], x_mx[0][1][:], x_words[0][:])
        nc.vector.reciprocal(out=inv_tp[:], in_=vec_cols[:, 0:P:ROWS])
        dst, src = side_by_side(w1_words[:, 0:64, :], w1_raw[:, :, 0:64])
        nc.vector.tensor_scalar(out=dst, in0=src, scalar1=-1.0, scalar2=None, op0=ALU.mult)
        dst, src = side_by_side(w1_words[:, 64:M, :], w1_raw[:, :, 64:M])
        nc.scalar.activation(out=dst, in_=src, func=ACT.Copy, scale=-1.0)
        quantize(nc, w_mx[0][0][:], w_mx[0][1][:], w2_words[:])
        quantize(nc, w_mx[1][0][:], w_mx[1][1][:], w1_words[:])
        nc.vector.tensor_tensor(out=ratio[:], in0=inv_tp[:], in1=vec_cols[:, 1:P:ROWS], op=ALU.mult)
        diff_matmuls(0)
        prepare(x_words[1], x_raw[1])
        clamp_and_exp(0, 0)
        quantize(nc, x_mx[1][0][:], x_mx[1][1][:], x_words[1][:])
        diff_matmuls(1)
        for g in range(1, G):
            clamp_and_exp(0, g)
        z2_matmuls(0)
        for g in groups:
            clamp_and_exp(1, g)
        z2_matmuls(1)

        base = [tile("base%d" % h, [P, G, HALF], F32) for h in halves]
        for h in halves:
            for g in groups:
                nc.vector.scalar_tensor_tensor(
                    out=base[h][:, g, :], in0=banks[g][h][:, 1, :], scalar=hs_col[g], in1=cq[h][:, g, :], op0=ALU.mult, op1=ALU.subtract
                )

        lg = [tile("lg%d" % h, [P, G, HALF], F32) for h in halves]
        hh_rows = [tile("hh_rows%d" % h, [P, PACK, HALF], BF16) for h in halves]
        for h in halves:
            for g in groups:
                nc.scalar.activation(out=lg[h][:, g, :], in_=e[h][:, g, :], func=ACT.Ln, bias=1.0)
                hh = tile("hh%d_%d" % (h, g), [P, HALF], BF16)
                nc.vector.scalar_tensor_tensor(
                    out=hh[:], in0=lg[h][:, g, :], scalar=ratio_col[g], in1=base[h][:, g, :], op0=ALU.mult, op1=ALU.add
                )
                nc.sync.dma_start(out=hh_rows[h][ROWS * g : ROWS * (g + 1), :, :], in_=hh[:])

        wo_words = tile("wo_words", [P, O, PACK], BF16)
        dst, src = side_by_side(wo_words[:], wo_raw[:])
        nc.scalar.copy(out=dst, in_=src)
        wo_mx = planes("wo", O)
        quantize(nc, wo_mx[0][:], wo_mx[1][:], wo_words[:])

        out_view = out.rearrange("g o n -> o g n")
        hh_words = [tile("hh_words%d" % h, [P, HALF, PACK], BF16) for h in halves]
        hh_mx = [planes("hh%d" % h, HALF) for h in halves]

        def second_layer(h):
            quantize(nc, hh_mx[h][0][:], hh_mx[h][1][:], hh_words[h][:])
            for c in range(0, HALF, NC):
                for g in groups:
                    row_tile_matmul(nc, banks[g][h][:, 0, c : c + NC], g, wo_mx, 0, hh_mx[h], c, True, True)

        def finish(h, g):
            cols = slice(h * HALF, (h + 1) * HALF)
            y = tile("y%d_%d" % (h, g), [P, HALF], F32)
            nc.vector.tensor_tensor(out=y[:], in0=banks[g][h][:, 0, :], in1=res_sb[:, g, cols], op=ALU.add)
            nc.sync.dma_start(out=out_view[:, g, cols], in_=y[:])

        def finish_off_vector(h, g):
            cols = slice(h * HALF, (h + 1) * HALF)
            y0 = tile("y0_%d_%d" % (h, g), [P, HALF], F32)
            y = tile("y%d_%d" % (h, g), [P, HALF], F32)
            nc.scalar.copy(out=y0[:], in_=banks[g][h][:, 0, :])
            nc.gpsimd.tensor_tensor(out=y[:], in0=y0[:], in1=res_sb[:, g, cols], op=ALU.add)
            return lambda: nc.scalar.dma_start(out=out_view[:, g, cols], in_=y[:])

        prepare(hh_words[0], hh_rows[0])
        second_layer(0)
        prepare(hh_words[1], hh_rows[1])
        second_layer(1)
        stores = [finish_off_vector(0, g) for g in (2, 3)]
        for store in stores:
            store()
        for g in (0, 1):
            finish(0, g)
        for g in groups:
            finish(1, g)
